import numpy as np, ml_dtypes
CORES = [40,64,80,88,96,104,120,144]
N = 8
import mx_ref
BF = ml_dtypes.bfloat16
def gentries(a):
    return np.ascontiguousarray(a.reshape(8, 16, -1).transpose(0, 2, 1)).reshape(8, -1)
def gtable(e):
    e = np.asarray(e); return np.ascontiguousarray(e.reshape(8, -1, 16).transpose(0, 2, 1)).reshape(128, -1).astype(np.int32)
def gcols(t, e):
    v = np.concatenate([t.reshape(8, 16, -1, 4), np.zeros((8, 16, 1, 4), BF)], axis=2)
    return np.ascontiguousarray(np.stack([v[g][:, e[g]] for g in range(8)])).reshape(128, -1)
def gpick(z, e):
    return np.concatenate([z[16 * g:16 * g + 16][:, e[g]] for g in range(8)])
def f(rng, *shape):
    return mx_ref.flush((rng.standard_normal(shape, dtype=np.float32) * np.exp2(rng.integers(-2, 3, shape[:-1] + (1,)))).astype(BF))
def wide(rng, *shape, cols=0):
    v = rng.standard_normal(shape, dtype=np.float32) * np.exp2(rng.integers(-12, 13, shape)).astype(np.float32)
    if cols: v *= np.repeat(np.exp2(rng.integers(-cols, cols + 1, shape[:-2] + (1, shape[-1] // 4))) * (rng.random(shape[:-2] + (1, shape[-1] // 4)) > 0.0625), 4, axis=-1).astype(np.float32)
    return mx_ref.flush(v.astype(BF))
T, CAPP, NB, KK = 512, 64, 2, 256
MASK = np.repeat(np.arange(128)[:, None] // 16 == np.arange(128)[None] // 16, 4, axis=1)
def lists(rng, agree=False, one=False, full=False, repeat=False):
    a, o = [], []
    for r in range(N):
        n = rng.integers(0, CAPP + 1, (8, N))
        far, most, none = -1, -1, -1
        if one:
            far = (r + rng.integers(1, N)) % N; most, none = rng.permutation(8)[:2]
            n[most, far] = CAPP; n[none, far] = 0
        if full: n[:] = CAPP
        n[n.sum(axis=1) == 0, r] = 1
        e = np.full((8, N, CAPP), -1)
        for g in range(8):
            for q in range(N):
                v = rng.integers(0, T, n[g, q])
                if one and g == most and q == far: v = rng.permutation(T)[:CAPP]
                if full: v[0] = 0; v[1] = T - 1
                e[g, q, rng.permutation(CAPP)[:n[g, q]]] = v
        if agree: e = np.stack([e[0]] * 8)
        e = e.reshape(8, -1); used = [np.flatnonzero(e[g] >= 0) for g in range(8)]
        k = np.stack([np.full(KK, rng.choice(u)) if repeat else rng.choice(u, KK) for u in used])
        if one: k[most, rng.permutation(KK)[:CAPP]] = far * CAPP + rng.permutation(CAPP)
        if full: k[:, 0] = 0; k[:, -1] = N * CAPP - 1
        a.append(gtable(e)); o.append(gtable(k))
    return {"rq": np.stack(a), "od": np.stack(o)}
def setup_inputs(rng):
    ky = f(rng, N, 128, 4 * T); qd = np.array(f(rng, N, 128, NB * 512))
    qd[:, ~np.concatenate([MASK] * NB, axis=1)] = 0
    return {"ky": ky, "qd": qd, **lists(rng)}
def setup_inputs_agree(rng):
    return {**setup_inputs(rng), **lists(rng, agree=True)}
def setup_inputs_one(rng):
    return {**setup_inputs(rng), **lists(rng, one=True)}
def setup_inputs_full(rng):
    return {**setup_inputs(rng), **lists(rng, full=True)}
def setup_inputs_repeat(rng):
    return {**setup_inputs(rng), **lists(rng, repeat=True)}
def setup_inputs_spread(rng):
    d = setup_inputs(rng); d["ky"] = wide(rng, N, 128, 4 * T, cols=8); return d
def check_inputs(d):
    b = []
    for r in range(N):
        e, o = gentries(d["rq"][r]), gentries(d["od"][r])
        if e.min() < -1 or e.max() >= T: b.append("rq")
        if o.min() < 0 or o.max() >= N * CAPP or (np.take_along_axis(e, np.clip(o, 0, N * CAPP - 1), axis=1) < 0).any(): b.append("od")
        if not (d["qd"][r][~np.concatenate([MASK] * NB, axis=1)].astype(np.float32) == 0).all(): b.append("qd")
    return b
def reference(ky, qd, rq, od):
    y = np.zeros((N, 128, NB * KK), np.float32)
    for r in range(N):
        e, o = gentries(rq[r]), gentries(od[r])
        slots = mx_ref.quantize(np.concatenate([gcols(ky[q], e[:, q * CAPP:(q + 1) * CAPP]) for q in range(N)], axis=1))
        for b in range(NB):
            z = mx_ref.matmul(mx_ref.quantize(np.ascontiguousarray(qd[r][:, 512 * b:512 * b + 512])), slots)
            y[r][:, KK * b:KK * b + KK] = gpick(z, o)
    return {"y": y}

@@ -1,0 +1,276 @@
+import comms_topo
+from concourse.bass import DstId, RemoteDMATransfer
+from concourse.mybir import dt, AluOpType, ActivationFunctionType
+
+N = 8
+W = 64
+LC = 4
+COPY = ActivationFunctionType.Copy
+
+SCRATCH = {
+    "rqi": ("sbuf", [128, 32], "int32"),
+    "lst": ("sbuf", [128, 32], "uint16"),
+    "offa": ("sbuf", [128, 12], "uint16"),
+    "offb0": ("sbuf", [128, 8], "uint16"),
+    "offb1": ("sbuf", [128, 8], "uint16"),
+    "hl": ("sbuf", [128, 32], "uint16"),
+    "kyt": ("sbuf", [128, 2048], "bfloat16"),
+    "kp0": ("sbuf", [128, 512], "bfloat16"),
+    "kp1": ("sbuf", [128, 512], "bfloat16"),
+    "kp2": ("sbuf", [128, 512], "bfloat16"),
+    "kp3": ("sbuf", [128, 512], "bfloat16"),
+    "ta": ("sbuf", [128, 1024], "bfloat16"),
+    "tb0": ("sbuf", [128, 512], "bfloat16"),
+    "tb1": ("sbuf", [128, 512], "bfloat16"),
+    "ca": ("sbuf", [128, 256], "float8_e4m3fn_x4"),
+    "pa": ("sbuf", [128, 256], "uint8"),
+    "cb0": ("sbuf", [128, 128], "float8_e4m3fn_x4"),
+    "pb0": ("sbuf", [128, 128], "uint8"),
+    "cb1": ("sbuf", [128, 128], "float8_e4m3fn_x4"),
+    "pb1": ("sbuf", [128, 128], "uint8"),
+    "hc": ("sbuf", [128, 128], "float8_e4m3fn_x4"),
+    "hp": ("sbuf", [128, 128], "uint8"),
+    "qt": ("sbuf", [128, 1024], "bfloat16"),
+    "qc": ("sbuf", [128, 256], "float8_e4m3fn_x4"),
+    "qp": ("sbuf", [128, 256], "uint8"),
+    "lc": ("sbuf", [128, 448], "float8_e4m3fn_x4"),
+    "lp": ("sbuf", [128, 448], "uint8"),
+    "ps": ("psum", [128, 4096], "float32"),
+    "z0": ("sbuf", [128, 512], "float32"),
+    "z1": ("sbuf", [128, 512], "float32"),
+    "odi": ("sbuf", [128, 16], "int32"),
+    "om": ("sbuf", [128, 128], "float32"),
+    "om2": ("sbuf", [128, 64], "float32"),
+    "om3": ("sbuf", [128, 32], "float32"),
+    "om4": ("sbuf", [128, 16], "float32"),
+    "offo": ("sbuf", [128, 16], "uint16"),
+    "y0": ("sbuf", [128, 256], "float32"),
+    "y1": ("sbuf", [128, 256], "float32"),
+}
+SEMAPHORES = [
+    "d_rq", "d_ky", "d_qd", "d_od", "d_y0", "d_y1",
+    "v_lst", "v_kp", "s_kp",
+    "v_go", "s_go", "v_ga", "s_ga", "v_gb0", "s_gb0", "v_gb1", "s_gb1",
+    "q_a", "q_b0", "q_b1", "q_q",
+    "o_1", "o_2", "o_3", "o_4", "o_5",
+    "t0_0", "t0_1", "t0_2", "t0_3", "t1_0", "t1_1", "t1_2", "t1_3",
+    "v_z", "s_z", "v_y", "s_y",
+    "la", "lb0", "lb1", "ra", "rb0", "rb1", "sent",
+    "h_l", "h_c", "h_p", "h_sent",
+]
+
+
+def order(core, T, topo):
+    me = T.rank_of(core)
+    cores = list(T.cores)
+    direct = [q for q in range(N) if q != me and topo.may_write(core, cores[q])]
+    cross = [q for q in range(N) if q != me and q not in direct]
+    j = sorted([me] + direct).index(me)
+    p0 = [q for i, q in enumerate(cross) if i // 2 == j // 2]
+    p1 = [q for i, q in enumerate(cross) if i // 2 != j // 2]
+    return [me] + direct + p0 + p1
+
+
+def helpers(core, T, topo):
+    o = order(core, T, topo)
+    cross = [list(T.cores)[q] for q in o[4:]]
+    ok = [h for h in topo.cores_of(core) if h != core and all(topo.may_write(h, d) for d in cross)]
+    return [[h for h in ok if topo.die(h) == topo.die(core)][0], [h for h in ok if topo.die(h) != topo.die(core)][0]]
+
+
+def runs(o):
+    n = max(max(o[4:6]) - min(o[4:6]), max(o[6:8]) - min(o[6:8])) + 1
+    return [min(min(o[4:6]), N - n), min(min(o[6:8]), N - n)], n
+
+
+def bits(es):
+    return sum(1 << e for e in es)
+
+
+def dst_id(topo, dst, src):
+    rid, pid = topo.addr(dst, src)
+    return DstId(rid=rid, pnc=pid)
+
+
+def helper_program(g, core, T, topo, owner, k):
+    cores = list(T.cores)
+    me = T.rank_of(owner)
+    o = order(owner, T, topo)
+    pair = o[4 + 2 * k:6 + 2 * k]
+    first, n = runs(o)
+    inner = topo.engines(owner, core)
+    n_in = len([e for e in inner if e not in topo.engines(core, cores[pair[0]])])
+    sent = 0
+
+    def send(pieces):
+        tr = []
+        for i, (q, src, dst, sem) in enumerate(pieces):
+            es = topo.engines(core, cores[q])
+            h = len(es) // 2
+            tr.append(RemoteDMATransfer(dst_ids=[dst_id(topo, cores[q], core)], dma_engine_mask=bits(es[i * h:i * h + h]),
+                                        remote_sem=sem, src=src, dst=dst))
+        g.remote_dma_fused(tr, local_sem=T.sem.h_sent)
+        return 2 * h
+
+    seat = [order(cores[q], T, topo).index(me) for q in pair]
+    g.wait_ge(T.sem.h_l, n_in // 2)
+    sent += send([(q, T.hl[:, LC * (q - first[k]):LC * (q - first[k]) + LC],
+                   T["offb%d" % k][:, LC * (s - 4 - 2 * k):LC * (s - 4 - 2 * k) + LC], T.sem["lb%d" % k])
+                  for q, s in zip(pair, seat)])
+    g.wait_ge(T.sem.h_c, n_in)
+    sent += send([(q, T.hc[:, W * i:W * i + W].bitcast(dt.uint8),
+                   T.lc[:, W * (s - 1):W * s].bitcast(dt.uint8), T.sem["rb%d" % k])
+                  for i, (q, s) in enumerate(zip(pair, seat))])
+    g.wait_ge(T.sem.h_p, n_in)
+    sent += send([(q, T.hp[:, W * i:W * i + W], T.lp[:, W * (s - 1):W * s], T.sem["rb%d" % k])
+                  for i, (q, s) in enumerate(zip(pair, seat))])
+    g.wait_ge(T.sem.h_sent, sent)
+
+
+def rank_program(g, core, T, topo):
+    cores = list(T.cores)
+    rank = T.rank_of(core)
+    if rank is None:
+        for owner in cores:
+            if core in topo.cores_of(owner):
+                hs = helpers(owner, T, topo)
+                if core in hs:
+                    helper_program(g, core, T, topo, owner, hs.index(core))
+        return
+
+    o = order(core, T, topo)
+    hs = helpers(core, T, topo)
+    seat = [order(cores[q], T, topo).index(rank) for q in o]
+    out_es = topo.engines(core, cores[o[1]])
+    in_es = [e for e in topo.engines(core, hs[0]) if e not in out_es]
+    S = T.sem
+
+    g.sync.dma_start(T.rqi[:], T.rq[:]).then_inc(S.d_rq, 16)
+    g.sync.dma_start(T.kyt[:, 0:1024], T.ky[:, 0:1024]).then_inc(S.d_ky, 16)
+    g.sync.wait_ge(S.la, 6)
+    g.sync.dma_start(T.qt[:], T.qd[:]).then_inc(S.d_qd, 16)
+    g.sync.dma_start(T.odi[:], T.od[:]).then_inc(S.d_od, 16)
+    g.sync.wait_ge(S.v_y, 1)
+    g.sync.dma_start(T.y[:, 0:256], T.y0[:]).then_inc(S.d_y0, 16)
+    g.sync.wait_ge(S.d_y0, 16)
+
+    sent = 0
+
+    def fused(trs, engines):
+        g.remote_dma_fused(trs, local_sem=S.sent)
+        return engines
+
+    first, n = runs(o)
+    g.wait_ge(S.v_lst, 1)
+    hq = len(in_es) // 2
+    sent += fused([RemoteDMATransfer(dst_ids=[dst_id(topo, hs[k], core)], dma_engine_mask=bits(in_es[k * hq:k * hq + hq]),
+                                     remote_sem=S.h_l, src=T.lst[:, LC * first[k]:LC * (first[k] + n)],
+                                     dst=T.hl[:, 0:LC * n]) for k in range(2)], 2 * hq)
+
+    def direct(src, dst, sem):
+        trs = []
+        for i in range(1, 4):
+            d = cores[o[i]]
+            trs.append(RemoteDMATransfer(dst_ids=[dst_id(topo, d, core)],
+                                         dma_engine_mask=bits(topo.engines(core, d)[2 * (i - 1):2 * i]),
+                                         remote_sem=sem, src=src(i), dst=dst(i)))
+        return fused(trs, 6)
+
+    sent += direct(lambda i: T.lst[:, LC * o[i]:LC * o[i] + LC],
+                   lambda i: T.offa[:, LC * (seat[i] - 1):LC * seat[i]], S.la)
+    g.wait_ge(S.q_a, 1)
+    sent += direct(lambda i: T.ca[:, W * i:W * i + W].bitcast(dt.uint8),
+                   lambda i: T.lc[:, W * (seat[i] - 1):W * seat[i]].bitcast(dt.uint8), S.ra)
+    sent += direct(lambda i: T.pa[:, W * i:W * i + W], lambda i: T.lp[:, W * (seat[i] - 1):W * seat[i]], S.ra)
+    for k in range(2):
+        rid, pid = topo.addr(hs[k], core)
+        g.wait_ge(S["q_b%d" % k], 1)
+        g.remote_dma(T.hc[:].bitcast(dt.uint8), T["cb%d" % k][:].bitcast(dt.uint8), S.h_c, S.sent, pid, rid, bits(in_es))
+        g.remote_dma(T.hp[:], T["pb%d" % k][:], S.h_p, S.sent, pid, rid, bits(in_es))
+        sent += 2 * len(in_es)
+    g.wait_ge(S.sent, sent)
+
+    v, sc, pe = g.vector, g.scalar, g.tensor
+    v.wait_ge(S.d_rq, 16)
+    v.tensor_copy(T.lst[:], T.rqi[:]).then_inc(S.v_lst, 1)
+    v.wait_ge(S.d_ky, 32)
+    for t in range(3):
+        v.tensor_copy(T["kp%d" % t][:], T.kyt[:, t:2048:4]).then_inc(S.v_kp, 1)
+
+    sc.dma_start(T.kyt[:, 1024:2048], T.ky[:, 1024:2048]).then_inc(S.d_ky, 16)
+    sc.wait_ge(S.d_ky, 32)
+    sc.activation(T.kp3[:], T.kyt[:, 3:2048:4], COPY).then_inc(S.s_kp, 1)
+
+    v.wait_ge(S.v_kp, 3)
+    v.wait_ge(S.v_lst, 1)
+    sc.wait_ge(S.v_kp, 3)
+    sc.wait_ge(S.v_lst, 1)
+    sc.wait_ge(S.s_kp, 1)
+
+    def gather(tile, a, b, offs, name):
+        for t in range(4):
+            out = T[tile][:, 4 * a + t:4 * b:4]
+            src = T["kp%d" % t][:, 0:512].indirect(offs)
+            if t < 2:
+                v.tensor_copy(out, src).then_inc(S["v_g" + name], 1)
+            else:
+                sc.activation(out, src, COPY).then_inc(S["s_g" + name], 1)
+
+    gather("ta", 0, W, T.lst[:, LC * rank:LC * rank + LC], "o")
+    v.wait_ge(S.la, 6)
+    sc.wait_ge(S.la, 6)
+    gather("ta", W, 4 * W, T.offa[:, 0:12], "a")
+    for s in ("v_go", "s_go", "v_ga", "s_ga"):
+        v.wait_ge(S[s], 2)
+    v.quantize_mx(T.ca[:], T.pa[:], T.ta[:]).then_inc(S.q_a, 1)
+    for k in range(2):
+        v.wait_ge(S["lb%d" % k], 8)
+        sc.wait_ge(S["lb%d" % k], 8)
+        gather("tb%d" % k, 0, 2 * W, T["offb%d" % k][:, 0:8], "b%d" % k)
+        v.wait_ge(S["v_gb%d" % k], 2)
+        v.wait_ge(S["s_gb%d" % k], 2)
+        v.quantize_mx(T["cb%d" % k][:], T["pb%d" % k][:], T["tb%d" % k][:]).then_inc(S["q_b%d" % k], 1)
+
+    v.wait_ge(S.d_qd, 16)
+    v.quantize_mx(T.qc[:], T.qp[:], T.qt[:]).then_inc(S.q_q, 1)
+    v.wait_ge(S.d_od, 16)
+    shift = [W * (o.index(q) - q) for q in range(N)]
+    v.tensor_scalar(T.om[:, 0:16], T.odi[:], float(shift[0]), None, AluOpType.add).then_inc(S.o_1, 1)
+    for q in range(1, N):
+        v.tensor_scalar(T.om[:, 16 * q:16 * q + 16], T.odi[:], float(W * q), float(shift[q] - shift[q - 1]),
+                        AluOpType.is_ge, AluOpType.mult).then_inc(S.o_1, 1)
+    v.wait_ge(S.o_1, 8)
+    v.tensor_tensor(T.om2[:], T.om[:, 0:64], T.om[:, 64:128], AluOpType.add).then_inc(S.o_2, 1)
+    v.wait_ge(S.o_2, 1)
+    v.tensor_tensor(T.om3[:], T.om2[:, 0:32], T.om2[:, 32:64], AluOpType.add).then_inc(S.o_3, 1)
+    v.wait_ge(S.o_3, 1)
+    v.tensor_tensor(T.om4[:], T.om3[:, 0:16], T.om3[:, 16:32], AluOpType.add).then_inc(S.o_4, 1)
+    v.wait_ge(S.o_4, 1)
+    v.tensor_copy(T.offo[:], T.om4[:]).then_inc(S.o_5, 1)
+
+    pieces = [("ca", "pa", 0, 2 * W), ("lc", "lp", 0, 3 * W), ("lc", "lp", 3 * W, 5 * W), ("lc", "lp", 5 * W, 7 * W)]
+    ready = [[("q_a", 1), ("q_q", 1)], [("ra", 12)], [("rb0", 16)], [("rb1", 16)]]
+    for j, (c, p, a, b) in enumerate(pieces):
+        for s, cnt in ready[j]:
+            pe.wait_ge(S[s], cnt)
+        for t in range(2):
+            bank = 512 * (4 * t + j)
+            pe.matmul_mx(T.ps[:, bank:bank + b - a], T.qc[:, 128 * t:128 * t + 128], T.qp[:, 128 * t:128 * t + 128],
+                         T[c][:, a:b], T[p][:, a:b], True, True).then_inc(S["t%d_%d" % (t, j)], 1)
+
+    at = [0, W, 4 * W, 6 * W, 8 * W]
+    for j in range(4):
+        w = at[j + 1] - at[j]
+        v.wait_ge(S["t0_%d" % j], 1)
+        v.tensor_copy(T.z0[:, at[j]:at[j + 1]], T.ps[:, 512 * j:512 * j + w]).then_inc(S.v_z, 1)
+        sc.wait_ge(S["t1_%d" % j], 1)
+        sc.activation(T.z1[:, at[j]:at[j + 1]], T.ps[:, 512 * (4 + j):512 * (4 + j) + w], COPY).then_inc(S.s_z, 1)
+    v.wait_ge(S.o_5, 1)
+    v.wait_ge(S.v_z, 4)
+    v.tensor_copy(T.y0[:], T.z0[:, 0:512].indirect(T.offo[:, 0:16])).then_inc(S.v_y, 1)
+    sc.wait_ge(S.o_5, 1)
+    sc.wait_ge(S.s_z, 4)
+    sc.activation(T.y1[:], T.z1[:, 0:512].indirect(T.offo[:, 0:16]), COPY).then_inc(S.s_y, 1)
+    sc.wait_ge(S.s_y, 1)
+    sc.dma_start(T.y[:, 256:512], T.y1[:]).then_inc(S.d_y1, 16)
+    sc.wait_ge(S.d_y1, 16)

@@ -1,6 +1,6 @@
 import comms_topo
 from concourse.bass import DstId, RemoteDMATransfer
-from concourse.mybir import dt, AluOpType, ActivationFunctionType
+from concourse.mybir import dt, ActivationFunctionType
 
 N = 8
 W = 64
@@ -8,122 +8,119 @@ LC = 4
 COPY = ActivationFunctionType.Copy
 
 SCRATCH = {
+    "dl": ("dram", [4, 128, LC], "int32"),
+    "hl": ("dram", [128, LC], "int32"),
     "rqi": ("sbuf", [128, 32], "int32"),
     "lst": ("sbuf", [128, 32], "uint16"),
-    "offa": ("sbuf", [128, 12], "uint16"),
-    "offb0": ("sbuf", [128, 8], "uint16"),
-    "offb1": ("sbuf", [128, 8], "uint16"),
-    "hl": ("sbuf", [128, 32], "uint16"),
+    "offd": ("sbuf", [128, LC], "uint16"),
+    "offi": ("sbuf", [128, 16], "int32"),
+    "off0": ("sbuf", [128, 8], "uint16"),
+    "off1": ("sbuf", [128, 8], "uint16"),
+    "off2": ("sbuf", [128, 8], "uint16"),
     "kyt": ("sbuf", [128, 2048], "bfloat16"),
     "kp0": ("sbuf", [128, 512], "bfloat16"),
     "kp1": ("sbuf", [128, 512], "bfloat16"),
     "kp2": ("sbuf", [128, 512], "bfloat16"),
     "kp3": ("sbuf", [128, 512], "bfloat16"),
-    "ta": ("sbuf", [128, 1024], "bfloat16"),
     "tb0": ("sbuf", [128, 512], "bfloat16"),
     "tb1": ("sbuf", [128, 512], "bfloat16"),
-    "ca": ("sbuf", [128, 256], "float8_e4m3fn_x4"),
-    "pa": ("sbuf", [128, 256], "uint8"),
+    "tb2": ("sbuf", [128, 1024], "bfloat16"),
     "cb0": ("sbuf", [128, 128], "float8_e4m3fn_x4"),
     "pb0": ("sbuf", [128, 128], "uint8"),
     "cb1": ("sbuf", [128, 128], "float8_e4m3fn_x4"),
     "pb1": ("sbuf", [128, 128], "uint8"),
-    "hc": ("sbuf", [128, 128], "float8_e4m3fn_x4"),
-    "hp": ("sbuf", [128, 128], "uint8"),
+    "cb2": ("sbuf", [128, 128], "float8_e4m3fn_x4"),
+    "pb2": ("sbuf", [128, 128], "uint8"),
+    "hc": ("sbuf", [128, 192], "float8_e4m3fn_x4"),
+    "hp": ("sbuf", [128, 192], "uint8"),
     "qt": ("sbuf", [128, 1024], "bfloat16"),
     "qc": ("sbuf", [128, 256], "float8_e4m3fn_x4"),
     "qp": ("sbuf", [128, 256], "uint8"),
-    "lc": ("sbuf", [128, 448], "float8_e4m3fn_x4"),
-    "lp": ("sbuf", [128, 448], "uint8"),
+    "lc": ("sbuf", [128, 576], "float8_e4m3fn_x4"),
+    "lp": ("sbuf", [128, 576], "uint8"),
     "ps": ("psum", [128, 4096], "float32"),
     "z0": ("sbuf", [128, 512], "float32"),
     "z1": ("sbuf", [128, 512], "float32"),
     "odi": ("sbuf", [128, 16], "int32"),
-    "om": ("sbuf", [128, 128], "float32"),
-    "om2": ("sbuf", [128, 64], "float32"),
-    "om3": ("sbuf", [128, 32], "float32"),
-    "om4": ("sbuf", [128, 16], "float32"),
     "offo": ("sbuf", [128, 16], "uint16"),
     "y0": ("sbuf", [128, 256], "float32"),
     "y1": ("sbuf", [128, 256], "float32"),
 }
 SEMAPHORES = [
-    "d_rq", "d_ky", "d_qd", "d_od", "d_y0", "d_y1",
-    "v_lst", "v_kp", "s_kp",
-    "v_go", "s_go", "v_ga", "s_ga", "v_gb0", "s_gb0", "v_gb1", "s_gb1",
-    "q_a", "q_b0", "q_b1", "q_q",
-    "o_1", "o_2", "o_3", "o_4", "o_5",
+    "d_l1", "d_l2", "d_rq", "d_ky0", "d_ky1", "d_qd", "d_od", "d_y0", "d_y1",
+    "v_lst", "v_l1", "v_l2", "v_od", "v_kp", "s_kp",
+    "v_g0", "s_g0", "v_g1", "s_g1", "v_g2", "s_g2", "v_gd", "s_gd", "v_go", "s_go",
+    "q_0", "q_1", "q_2", "q_d", "q_q",
     "t0_0", "t0_1", "t0_2", "t0_3", "t1_0", "t1_1", "t1_2", "t1_3",
-    "v_z", "s_z", "v_y", "s_y",
-    "la", "lb0", "lb1", "ra", "rb0", "rb1", "sent",
-    "h_l", "h_c", "h_p", "h_sent",
+    "v_z", "s_z", "v_y0", "s_y0", "v_y1", "s_y1",
+    "l0", "l1", "l2", "ld", "r0", "r1", "r2", "rd", "sent",
+    "h_l", "h_0", "h_1", "h_2", "h_sent",
 ]
 
 
 def order(core, T, topo):
     me = T.rank_of(core)
     cores = list(T.cores)
-    direct = [q for q in range(N) if q != me and topo.may_write(core, cores[q])]
-    cross = [q for q in range(N) if q != me and q not in direct]
-    j = sorted([me] + direct).index(me)
-    p0 = [q for i, q in enumerate(cross) if i // 2 == j // 2]
-    p1 = [q for i, q in enumerate(cross) if i // 2 != j // 2]
-    return [me] + direct + p0 + p1
+    same = [q for q in range(N) if q == me or topo.may_write(core, cores[q])]
+    cross = [q for q in range(N) if q not in same]
+    j = same.index(me)
+    return [same[j ^ x] for x in range(4)] + [cross[j ^ x] for x in range(4)]
 
 
 def helpers(core, T, topo):
-    o = order(core, T, topo)
-    cross = [list(T.cores)[q] for q in o[4:]]
-    ok = [h for h in topo.cores_of(core) if h != core and all(topo.may_write(h, d) for d in cross)]
-    return [[h for h in ok if topo.die(h) == topo.die(core)][0], [h for h in ok if topo.die(h) != topo.die(core)][0]]
+    far = [list(T.cores)[q] for q in order(core, T, topo)[4:]]
+    ok = [h for h in topo.cores_of(core) if h != core and all(topo.may_write(h, d) for d in far)]
+    return [[h for h in ok if topo.die(h) == topo.die(core)], [h for h in ok if topo.die(h) != topo.die(core)]]
 
 
-def runs(o):
-    n = max(max(o[4:6]) - min(o[4:6]), max(o[6:8]) - min(o[6:8])) + 1
-    return [min(min(o[4:6]), N - n), min(min(o[6:8]), N - n)], n
+def engine_sets(core, T, topo):
+    out_es = topo.engines(core, list(T.cores)[order(core, T, topo)[1]])
+    return out_es, [e for e in topo.engines(core, helpers(core, T, topo)[0][0]) if e not in out_es]
 
 
 def bits(es):
     return sum(1 << e for e in es)
 
 
-def dst_id(topo, dst, src):
-    rid, pid = topo.addr(dst, src)
-    return DstId(rid=rid, pnc=pid)
+def transfer(topo, core, dst_core, es, sem, src, dst):
+    rid, pid = topo.addr(dst_core, core)
+    return RemoteDMATransfer(dst_ids=[DstId(rid=rid, pnc=pid)], dma_engine_mask=bits(es), remote_sem=sem, src=src, dst=dst)
 
 
-def helper_program(g, core, T, topo, owner, k):
+def codes(buf, i):
+    return buf[:, W * i:W * i + W].bitcast(dt.uint8)
+
+
+def plane(buf, i):
+    return buf[:, W * i:W * i + W]
+
+
+def carries_codes(x, b):
+    return (x == 0) == (b > 0)
+
+
+def helper_program(g, core, T, topo, owner, side, x):
     cores = list(T.cores)
-    me = T.rank_of(owner)
     o = order(owner, T, topo)
-    pair = o[4 + 2 * k:6 + 2 * k]
-    first, n = runs(o)
-    inner = topo.engines(owner, core)
-    n_in = len([e for e in inner if e not in topo.engines(core, cores[pair[0]])])
+    n_in = len(engine_sets(owner, T, topo)[side])
     sent = 0
 
-    def send(pieces):
-        tr = []
-        for i, (q, src, dst, sem) in enumerate(pieces):
-            es = topo.engines(core, cores[q])
-            h = len(es) // 2
-            tr.append(RemoteDMATransfer(dst_ids=[dst_id(topo, cores[q], core)], dma_engine_mask=bits(es[i * h:i * h + h]),
-                                        remote_sem=sem, src=src, dst=dst))
-        g.remote_dma_fused(tr, local_sem=T.sem.h_sent)
-        return 2 * h
+    def send(place, dst, src, sem):
+        d = cores[o[place]]
+        rid, pid = topo.addr(d, core)
+        g.remote_dma(dst, src, sem, T.sem.h_sent, pid, rid, topo.mask(core, d))
+        return len(topo.engines(core, d))
 
-    seat = [order(cores[q], T, topo).index(me) for q in pair]
-    g.wait_ge(T.sem.h_l, n_in // 2)
-    sent += send([(q, T.hl[:, LC * (q - first[k]):LC * (q - first[k]) + LC],
-                   T["offb%d" % k][:, LC * (s - 4 - 2 * k):LC * (s - 4 - 2 * k) + LC], T.sem["lb%d" % k])
-                  for q, s in zip(pair, seat)])
-    g.wait_ge(T.sem.h_c, n_in)
-    sent += send([(q, T.hc[:, W * i:W * i + W].bitcast(dt.uint8),
-                   T.lc[:, W * (s - 1):W * s].bitcast(dt.uint8), T.sem["rb%d" % k])
-                  for i, (q, s) in enumerate(zip(pair, seat))])
-    g.wait_ge(T.sem.h_p, n_in)
-    sent += send([(q, T.hp[:, W * i:W * i + W], T.lp[:, W * (s - 1):W * s], T.sem["rb%d" % k])
-                  for i, (q, s) in enumerate(zip(pair, seat))])
+    i = 2 * x + side
+    g.wait_ge(T.sem.h_l, 1)
+    sent += send(4 + i, T.offi[:, LC * i:LC * i + LC], T.hl[:], T.sem["l%d" % (1 + x)])
+    for b in range(3):
+        place = 2 + 2 * b + side
+        g.wait_ge(T.sem["h_%d" % b], n_in)
+        if carries_codes(x, b):
+            sent += send(place, codes(T.lc, place + 1), codes(T.hc, b), T.sem["r%d" % b])
+        else:
+            sent += send(place, plane(T.lp, place + 1), plane(T.hp, b), T.sem["r%d" % b])
     g.wait_ge(T.sem.h_sent, sent)
 
 
@@ -134,81 +131,81 @@ def rank_program(g, core, T, topo):
         for owner in cores:
             if core in topo.cores_of(owner):
                 hs = helpers(owner, T, topo)
-                if core in hs:
-                    helper_program(g, core, T, topo, owner, hs.index(core))
+                for side in range(2):
+                    if core in hs[side]:
+                        helper_program(g, core, T, topo, owner, side, hs[side].index(core))
         return
 
     o = order(core, T, topo)
     hs = helpers(core, T, topo)
-    seat = [order(cores[q], T, topo).index(rank) for q in o]
-    out_es = topo.engines(core, cores[o[1]])
-    in_es = [e for e in topo.engines(core, hs[0]) if e not in out_es]
+    sides = engine_sets(core, T, topo)
+    out_es, in_es = sides
+    n_out, hq = len(out_es), len(in_es) // 2
     S = T.sem
+    v, sc, pe, sy = g.vector, g.scalar, g.tensor, g.sync
 
-    g.sync.dma_start(T.rqi[:], T.rq[:]).then_inc(S.d_rq, 16)
-    g.sync.dma_start(T.kyt[:, 0:1024], T.ky[:, 0:1024]).then_inc(S.d_ky, 16)
-    g.sync.wait_ge(S.la, 6)
-    g.sync.dma_start(T.qt[:], T.qd[:]).then_inc(S.d_qd, 16)
-    g.sync.dma_start(T.odi[:], T.od[:]).then_inc(S.d_od, 16)
-    g.sync.wait_ge(S.v_y, 1)
-    g.sync.dma_start(T.y[:, 0:256], T.y0[:]).then_inc(S.d_y0, 16)
-    g.sync.wait_ge(S.d_y0, 16)
+    def park(queue, i):
+        q = o[4 + i]
+        queue.dma_start(T.dl[i], T.rq[:, LC * q:LC * q + LC]).then_inc(S["d_l%d" % (1 + i // 2)], 16)
 
-    sent = 0
+    park(sy, 0)
+    park(sc, 1)
+    park(sy, 2)
+    park(sc, 3)
+    sc.dma_start(T.rqi[:], T.rq[:]).then_inc(S.d_rq, 16)
+    sy.dma_start(T.kyt[:, 0:1024], T.ky[:, 0:1024]).then_inc(S.d_ky0, 16)
+    sy.dma_start(T.kyt[:, 1024:2048], T.ky[:, 1024:2048]).then_inc(S.d_ky1, 16)
+    sy.wait_ge(S.l0, n_out)
+    sy.dma_start(T.qt[:], T.qd[:]).then_inc(S.d_qd, 16)
+    sy.dma_start(T.odi[:], T.od[:]).then_inc(S.d_od, 16)
 
-    def fused(trs, engines):
-        g.remote_dma_fused(trs, local_sem=S.sent)
-        return engines
+    sent = [0]
 
-    first, n = runs(o)
+    def fused(*moves):
+        g.remote_dma_fused([transfer(topo, core, *m) for m in moves], local_sem=S.sent)
+        sent[0] += sum(len(m[1]) for m in moves)
+
+    def lists_in(x):
+        g.wait_ge(S["d_l%d" % (1 + x)], 32)
+        fused(*[(hs[side][x], [in_es[hq * side + 2 * x]], S.h_l, T.dl[2 * x + side], T.hl[:]) for side in range(2)])
+
+    def own_list(place):
+        return T.lst[:, LC * o[place]:LC * o[place] + LC]
+
+    lists_in(0)
+    lists_in(1)
     g.wait_ge(S.v_lst, 1)
-    hq = len(in_es) // 2
-    sent += fused([RemoteDMATransfer(dst_ids=[dst_id(topo, hs[k], core)], dma_engine_mask=bits(in_es[k * hq:k * hq + hq]),
-                                     remote_sem=S.h_l, src=T.lst[:, LC * first[k]:LC * (first[k] + n)],
-                                     dst=T.hl[:, 0:LC * n]) for k in range(2)], 2 * hq)
+    fused(*[(cores[o[2 + i]], out_es[i * n_out // 2:(i + 1) * n_out // 2], S.l0, own_list(2 + i),
+             T.off0[:, LC * i:LC * i + LC]) for i in range(2)])
+    fused((cores[o[1]], out_es, S.ld, own_list(1), T.offd[:]))
+    for b in range(3):
+        xc = 0 if carries_codes(0, b) else 1
+        g.wait_ge(S["q_%d" % b], 1)
+        fused(*[(hs[side][xc], sides[side], S["h_%d" % b], codes(T["cb%d" % b], side), codes(T.hc, b)) for side in range(2)])
+        fused(*[(hs[side][1 - xc], sides[side], S["h_%d" % b], plane(T["pb%d" % b], side), plane(T.hp, b))
+                for side in range(2)])
+    g.wait_ge(S.q_d, 1)
+    fused((cores[o[1]], out_es, S.rd, codes(T.lc, 0), codes(T.lc, 2)))
+    fused((cores[o[1]], out_es, S.rd, plane(T.lp, 0), plane(T.lp, 2)))
+    g.wait_ge(S.sent, sent[0])
 
-    def direct(src, dst, sem):
-        trs = []
-        for i in range(1, 4):
-            d = cores[o[i]]
-            trs.append(RemoteDMATransfer(dst_ids=[dst_id(topo, d, core)],
-                                         dma_engine_mask=bits(topo.engines(core, d)[2 * (i - 1):2 * i]),
-                                         remote_sem=sem, src=src(i), dst=dst(i)))
-        return fused(trs, 6)
-
-    sent += direct(lambda i: T.lst[:, LC * o[i]:LC * o[i] + LC],
-                   lambda i: T.offa[:, LC * (seat[i] - 1):LC * seat[i]], S.la)
-    g.wait_ge(S.q_a, 1)
-    sent += direct(lambda i: T.ca[:, W * i:W * i + W].bitcast(dt.uint8),
-                   lambda i: T.lc[:, W * (seat[i] - 1):W * seat[i]].bitcast(dt.uint8), S.ra)
-    sent += direct(lambda i: T.pa[:, W * i:W * i + W], lambda i: T.lp[:, W * (seat[i] - 1):W * seat[i]], S.ra)
-    for k in range(2):
-        rid, pid = topo.addr(hs[k], core)
-        g.wait_ge(S["q_b%d" % k], 1)
-        g.remote_dma(T.hc[:].bitcast(dt.uint8), T["cb%d" % k][:].bitcast(dt.uint8), S.h_c, S.sent, pid, rid, bits(in_es))
-        g.remote_dma(T.hp[:], T["pb%d" % k][:], S.h_p, S.sent, pid, rid, bits(in_es))
-        sent += 2 * len(in_es)
-    g.wait_ge(S.sent, sent)
-
-    v, sc, pe = g.vector, g.scalar, g.tensor
     v.wait_ge(S.d_rq, 16)
     v.tensor_copy(T.lst[:], T.rqi[:]).then_inc(S.v_lst, 1)
-    v.wait_ge(S.d_ky, 32)
-    for t in range(3):
-        v.tensor_copy(T["kp%d" % t][:], T.kyt[:, t:2048:4]).then_inc(S.v_kp, 1)
 
-    sc.dma_start(T.kyt[:, 1024:2048], T.ky[:, 1024:2048]).then_inc(S.d_ky, 16)
-    sc.wait_ge(S.d_ky, 32)
-    sc.activation(T.kp3[:], T.kyt[:, 3:2048:4], COPY).then_inc(S.s_kp, 1)
+    for h in range(2):
+        v.wait_ge(S["d_ky%d" % h], 16)
+        for t in range(3):
+            v.tensor_copy(T["kp%d" % t][:, 256 * h:256 * h + 256],
+                          T.kyt[:, 1024 * h + t:1024 * h + 1024:4]).then_inc(S.v_kp, 1)
+        sc.wait_ge(S["d_ky%d" % h], 16)
+        sc.activation(T.kp3[:, 256 * h:256 * h + 256], T.kyt[:, 1024 * h + 3:1024 * h + 1024:4], COPY).then_inc(S.s_kp, 1)
 
-    v.wait_ge(S.v_kp, 3)
-    v.wait_ge(S.v_lst, 1)
-    sc.wait_ge(S.v_kp, 3)
-    sc.wait_ge(S.v_lst, 1)
-    sc.wait_ge(S.s_kp, 1)
+    v.wait_ge(S.v_kp, 6)
+    sc.wait_ge(S.v_kp, 6)
+    sc.wait_ge(S.s_kp, 2)
 
-    def gather(tile, a, b, offs, name):
-        for t in range(4):
+    def gather(tile, a, b, offs, name, ts=range(4)):
+        for t in ts:
             out = T[tile][:, 4 * a + t:4 * b:4]
             src = T["kp%d" % t][:, 0:512].indirect(offs)
             if t < 2:
@@ -216,61 +213,68 @@ def rank_program(g, core, T, topo):
             else:
                 sc.activation(out, src, COPY).then_inc(S["s_g" + name], 1)
 
-    gather("ta", 0, W, T.lst[:, LC * rank:LC * rank + LC], "o")
-    v.wait_ge(S.la, 6)
-    sc.wait_ge(S.la, 6)
-    gather("ta", W, 4 * W, T.offa[:, 0:12], "a")
-    for s in ("v_go", "s_go", "v_ga", "s_ga"):
-        v.wait_ge(S[s], 2)
-    v.quantize_mx(T.ca[:], T.pa[:], T.ta[:]).then_inc(S.q_a, 1)
-    for k in range(2):
-        v.wait_ge(S["lb%d" % k], 8)
-        sc.wait_ge(S["lb%d" % k], 8)
-        gather("tb%d" % k, 0, 2 * W, T["offb%d" % k][:, 0:8], "b%d" % k)
-        v.wait_ge(S["v_gb%d" % k], 2)
-        v.wait_ge(S["s_gb%d" % k], 2)
-        v.quantize_mx(T["cb%d" % k][:], T["pb%d" % k][:], T["tb%d" % k][:]).then_inc(S["q_b%d" % k], 1)
+    def cast(b):
+        v.wait_ge(S["l%d" % b], 2 * n_out)
+        v.tensor_copy(T["off%d" % b][:], T.offi[:, 8 * b - 8:8 * b]).then_inc(S["v_l%d" % b], 1)
 
+    def both_wait(sem, n):
+        v.wait_ge(sem, n)
+        sc.wait_ge(sem, n)
+
+    def quantise(name, c, p, tile, a):
+        v.wait_ge(S["v_g" + name], 2)
+        v.wait_ge(S["s_g" + name], 2)
+        v.quantize_mx(T[c][:, 0:2 * W], T[p][:, 0:2 * W], T[tile][:, 4 * a:4 * a + 8 * W]).then_inc(S["q_" + name], 1)
+
+    both_wait(S.l0, n_out)
+    gather("tb0", 0, 2 * W, T.off0[:], "0")
+    quantise("0", "cb0", "pb0", "tb0", 0)
+    both_wait(S.v_lst, 1)
+    gather("tb2", 3 * W, 4 * W, own_list(0), "o")
+    cast(1)
+    both_wait(S.v_l1, 1)
+    gather("tb1", 0, 2 * W, T.off1[:], "1")
+    cast(2)
+    quantise("1", "cb1", "pb1", "tb1", 0)
+    both_wait(S.v_l2, 1)
+    gather("tb2", 0, 2 * W, T.off2[:], "2")
+    quantise("2", "cb2", "pb2", "tb2", 0)
+    both_wait(S.ld, n_out)
+    gather("tb2", 2 * W, 3 * W, T.offd[:], "d")
+    v.wait_ge(S.v_go, 2)
+    v.wait_ge(S.s_go, 2)
+    quantise("d", "lc", "lp", "tb2", 2 * W)
     v.wait_ge(S.d_qd, 16)
     v.quantize_mx(T.qc[:], T.qp[:], T.qt[:]).then_inc(S.q_q, 1)
     v.wait_ge(S.d_od, 16)
-    shift = [W * (o.index(q) - q) for q in range(N)]
-    v.tensor_scalar(T.om[:, 0:16], T.odi[:], float(shift[0]), None, AluOpType.add).then_inc(S.o_1, 1)
-    for q in range(1, N):
-        v.tensor_scalar(T.om[:, 16 * q:16 * q + 16], T.odi[:], float(W * q), float(shift[q] - shift[q - 1]),
-                        AluOpType.is_ge, AluOpType.mult).then_inc(S.o_1, 1)
-    v.wait_ge(S.o_1, 8)
-    v.tensor_tensor(T.om2[:], T.om[:, 0:64], T.om[:, 64:128], AluOpType.add).then_inc(S.o_2, 1)
-    v.wait_ge(S.o_2, 1)
-    v.tensor_tensor(T.om3[:], T.om2[:, 0:32], T.om2[:, 32:64], AluOpType.add).then_inc(S.o_3, 1)
-    v.wait_ge(S.o_3, 1)
-    v.tensor_tensor(T.om4[:], T.om3[:, 0:16], T.om3[:, 16:32], AluOpType.add).then_inc(S.o_4, 1)
-    v.wait_ge(S.o_4, 1)
-    v.tensor_copy(T.offo[:], T.om4[:]).then_inc(S.o_5, 1)
+    v.tensor_copy(T.offo[:], T.odi[:]).then_inc(S.v_od, 1)
 
-    pieces = [("ca", "pa", 0, 2 * W), ("lc", "lp", 0, 3 * W), ("lc", "lp", 3 * W, 5 * W), ("lc", "lp", 5 * W, 7 * W)]
-    ready = [[("q_a", 1), ("q_q", 1)], [("ra", 12)], [("rb0", 16)], [("rb1", 16)]]
-    for j, (c, p, a, b) in enumerate(pieces):
-        for s, cnt in ready[j]:
+    pe.wait_ge(S.q_q, 1)
+    steps = [(2, [("r0", 4 * n_out)]), (4, [("r1", 4 * n_out)]), (0, [("q_d", 1), ("rd", 2 * n_out)]), (6, [("r2", 4 * n_out)])]
+    for j, (place, ready) in enumerate(steps):
+        a = W * (place + 1)
+        for s, cnt in ready:
             pe.wait_ge(S[s], cnt)
         for t in range(2):
             bank = 512 * (4 * t + j)
-            pe.matmul_mx(T.ps[:, bank:bank + b - a], T.qc[:, 128 * t:128 * t + 128], T.qp[:, 128 * t:128 * t + 128],
-                         T[c][:, a:b], T[p][:, a:b], True, True).then_inc(S["t%d_%d" % (t, j)], 1)
-
-    at = [0, W, 4 * W, 6 * W, 8 * W]
-    for j in range(4):
-        w = at[j + 1] - at[j]
+            pe.matmul_mx(T.ps[:, bank:bank + 2 * W], T.qc[:, 128 * t:128 * t + 128], T.qp[:, 128 * t:128 * t + 128],
+                         T.lc[:, a:a + 2 * W], T.lp[:, a:a + 2 * W], True, True).then_inc(S["t%d_%d" % (t, j)], 1)
         v.wait_ge(S["t0_%d" % j], 1)
-        v.tensor_copy(T.z0[:, at[j]:at[j + 1]], T.ps[:, 512 * j:512 * j + w]).then_inc(S.v_z, 1)
         sc.wait_ge(S["t1_%d" % j], 1)
-        sc.activation(T.z1[:, at[j]:at[j + 1]], T.ps[:, 512 * (4 + j):512 * (4 + j) + w], COPY).then_inc(S.s_z, 1)
-    v.wait_ge(S.o_5, 1)
-    v.wait_ge(S.v_z, 4)
-    v.tensor_copy(T.y0[:], T.z0[:, 0:512].indirect(T.offo[:, 0:16])).then_inc(S.v_y, 1)
-    sc.wait_ge(S.o_5, 1)
-    sc.wait_ge(S.s_z, 4)
-    sc.activation(T.y1[:], T.z1[:, 0:512].indirect(T.offo[:, 0:16]), COPY).then_inc(S.s_y, 1)
-    sc.wait_ge(S.s_y, 1)
-    sc.dma_start(T.y[:, 256:512], T.y1[:]).then_inc(S.d_y1, 16)
-    sc.wait_ge(S.d_y1, 16)
+        for i in range(2):
+            q = o[place + i]
+            v.tensor_copy(T.z0[:, W * q:W * q + W], T.ps[:, 512 * j + W * i:512 * j + W * i + W]).then_inc(S.v_z, 1)
+            sc.activation(T.z1[:, W * q:W * q + W], T.ps[:, 512 * (4 + j) + W * i:512 * (4 + j) + W * i + W],
+                          COPY).then_inc(S.s_z, 1)
+
+    both_wait(S.v_od, 1)
+    for t, zs in enumerate((S.v_z, S.s_z)):
+        z, y = T["z%d" % t], T["y%d" % t]
+        both_wait(zs, N)
+        v.tensor_copy(y[:, 0:128], z[:, 0:512].indirect(T.offo[:, 0:8])).then_inc(S["v_y%d" % t], 1)
+        sc.activation(y[:, 128:256], z[:, 0:512].indirect(T.offo[:, 8:16]), COPY).then_inc(S["s_y%d" % t], 1)
+    for t, queue in enumerate((sy, sc)):
+        queue.wait_ge(S["v_y%d" % t], 1)
+        queue.wait_ge(S["s_y%d" % t], 1)
+        queue.dma_start(T.y[:, 256 * t:256 * t + 256], T["y%d" % t][:]).then_inc(S["d_y%d" % t], 16)
+        queue.wait_ge(S["d_y%d" % t], 16)

@@ -9,11 +9,11 @@ COPY = ActivationFunctionType.Copy
 
 SCRATCH = {
     "dl": ("dram", [4, 128, LC], "int32"),
-    "hl": ("dram", [128, LC], "int32"),
+    "hl": ("dram", [2, 128, LC], "int32"),
     "rqi": ("sbuf", [128, 32], "int32"),
     "lst": ("sbuf", [128, 32], "uint16"),
-    "offd": ("sbuf", [128, LC], "uint16"),
     "offi": ("sbuf", [128, 16], "int32"),
+    "offd": ("sbuf", [128, LC], "uint16"),
     "off0": ("sbuf", [128, 8], "uint16"),
     "off1": ("sbuf", [128, 8], "uint16"),
     "off2": ("sbuf", [128, 8], "uint16"),
@@ -25,6 +25,8 @@ SCRATCH = {
     "tb0": ("sbuf", [128, 512], "bfloat16"),
     "tb1": ("sbuf", [128, 512], "bfloat16"),
     "tb2": ("sbuf", [128, 1024], "bfloat16"),
+    "cd": ("sbuf", [128, 128], "float8_e4m3fn_x4"),
+    "pd": ("sbuf", [128, 128], "uint8"),
     "cb0": ("sbuf", [128, 128], "float8_e4m3fn_x4"),
     "pb0": ("sbuf", [128, 128], "uint8"),
     "cb1": ("sbuf", [128, 128], "float8_e4m3fn_x4"),
@@ -50,11 +52,11 @@ SEMAPHORES = [
     "d_l1", "d_l2", "d_rq", "d_ky0", "d_ky1", "d_qd", "d_od", "d_y0", "d_y1",
     "v_lst", "v_l1", "v_l2", "v_od", "v_kp", "s_kp",
     "v_g0", "s_g0", "v_g1", "s_g1", "v_g2", "s_g2", "v_gd", "s_gd", "v_go", "s_go",
-    "q_0", "q_1", "q_2", "q_d", "q_q",
+    "q_0", "q_1", "q_2", "q_d", "q_o", "q_q",
     "t0_0", "t0_1", "t0_2", "t0_3", "t1_0", "t1_1", "t1_2", "t1_3",
     "v_z", "s_z", "v_y0", "s_y0", "v_y1", "s_y1",
     "l0", "l1", "l2", "ld", "r0", "r1", "r2", "rd", "sent",
-    "h_l", "h_0", "h_1", "h_2", "h_sent",
+    "h_l1", "h_l2", "h_c0", "h_c1", "h_c2", "h_p0", "h_p1", "h_p2", "h_sent",
 ]
 
 
@@ -70,7 +72,8 @@ def order(core, T, topo):
 def helpers(core, T, topo):
     far = [list(T.cores)[q] for q in order(core, T, topo)[4:]]
     ok = [h for h in topo.cores_of(core) if h != core and all(topo.may_write(h, d) for d in far)]
-    return [[h for h in ok if topo.die(h) == topo.die(core)], [h for h in ok if topo.die(h) != topo.die(core)]]
+    rest = [h for h in topo.cores_of(core) if h != core and h not in ok and topo.die(h) == topo.die(core)]
+    return [[h for h in ok if topo.die(h) == topo.die(core)], [h for h in ok if topo.die(h) != topo.die(core)], rest]
 
 
 def engine_sets(core, T, topo):
@@ -95,14 +98,18 @@ def plane(buf, i):
     return buf[:, W * i:W * i + W]
 
 
-def carries_codes(x, b):
-    return (x == 0) == (b > 0)
+WAY = ((((1, 0), (1, 1)), ((2, 0), (2, 0))),
+       (((1, 0), (1, 1)), ((0, 0), (0, 1))),
+       (((1, 0), (1, 1)), ((0, 0), (0, 1))))
+CALLS = (((1, (0,)), (0, (0,)), (0, (1,)), (1, (1,))),
+         ((0, (0, 1)), (1, (0, 1))),
+         ((0, (0,)), (1, (0,)), (0, (1,)), (1, (1,))))
 
 
 def helper_program(g, core, T, topo, owner, side, x):
     cores = list(T.cores)
     o = order(owner, T, topo)
-    n_in = len(engine_sets(owner, T, topo)[side])
+    n_all = len(topo.engines(owner, core))
     sent = 0
 
     def send(place, dst, src, sem):
@@ -111,16 +118,19 @@ def helper_program(g, core, T, topo, owner, side, x):
         g.remote_dma(dst, src, sem, T.sem.h_sent, pid, rid, topo.mask(core, d))
         return len(topo.engines(core, d))
 
-    i = 2 * x + side
-    g.wait_ge(T.sem.h_l, 1)
-    sent += send(4 + i, T.offi[:, LC * i:LC * i + LC], T.hl[:], T.sem["l%d" % (1 + x)])
+    if side == 0:
+        for b in (1, 2):
+            i = 2 * b - 2 + x
+            g.wait_ge(T.sem["h_l%d" % b], 1)
+            sent += send(4 + i, T.offi[:, LC * i:LC * i + LC], T.hl[b - 1], T.sem["l%d" % b])
     for b in range(3):
-        place = 2 + 2 * b + side
-        g.wait_ge(T.sem["h_%d" % b], n_in)
-        if carries_codes(x, b):
-            sent += send(place, codes(T.lc, place + 1), codes(T.hc, b), T.sem["r%d" % b])
-        else:
-            sent += send(place, plane(T.lp, place + 1), plane(T.hp, b), T.sem["r%d" % b])
+        for kind, ranks in CALLS[b]:
+            view, held, landing = ((codes, T.hc, T.lc), (plane, T.hp, T.lp))[kind]
+            for i in ranks:
+                if WAY[b][i][kind] == (side, x):
+                    place = 2 + 2 * b + i
+                    g.wait_ge(T.sem["h_%s%d" % ("cp"[kind], b)], n_all // len(ranks))
+                    sent += send(place, view(landing, place + 1), view(held, b), T.sem["r%d" % b])
     g.wait_ge(T.sem.h_sent, sent)
 
 
@@ -131,7 +141,7 @@ def rank_program(g, core, T, topo):
         for owner in cores:
             if core in topo.cores_of(owner):
                 hs = helpers(owner, T, topo)
-                for side in range(2):
+                for side in range(3):
                     if core in hs[side]:
                         helper_program(g, core, T, topo, owner, side, hs[side].index(core))
         return
@@ -150,11 +160,11 @@ def rank_program(g, core, T, topo):
 
     park(sy, 0)
     park(sc, 1)
-    park(sy, 2)
-    park(sc, 3)
-    sc.dma_start(T.rqi[:], T.rq[:]).then_inc(S.d_rq, 16)
-    sy.dma_start(T.kyt[:, 0:1024], T.ky[:, 0:1024]).then_inc(S.d_ky0, 16)
+    sy.dma_start(T.rqi[:], T.rq[:]).then_inc(S.d_rq, 16)
+    sc.dma_start(T.kyt[:, 0:1024], T.ky[:, 0:1024]).then_inc(S.d_ky0, 16)
     sy.dma_start(T.kyt[:, 1024:2048], T.ky[:, 1024:2048]).then_inc(S.d_ky1, 16)
+    park(sy, 2)
+    park(sy, 3)
     sy.wait_ge(S.l0, n_out)
     sy.dma_start(T.qt[:], T.qd[:]).then_inc(S.d_qd, 16)
     sy.dma_start(T.odi[:], T.od[:]).then_inc(S.d_od, 16)
@@ -165,28 +175,29 @@ def rank_program(g, core, T, topo):
         g.remote_dma_fused([transfer(topo, core, *m) for m in moves], local_sem=S.sent)
         sent[0] += sum(len(m[1]) for m in moves)
 
-    def lists_in(x):
-        g.wait_ge(S["d_l%d" % (1 + x)], 32)
-        fused(*[(hs[side][x], [in_es[hq * side + 2 * x]], S.h_l, T.dl[2 * x + side], T.hl[:]) for side in range(2)])
-
     def own_list(place):
         return T.lst[:, LC * o[place]:LC * o[place] + LC]
 
-    lists_in(0)
+    def lists_in(b):
+        g.wait_ge(S["d_l%d" % b], 32)
+        fused(*[(hs[0][x], [in_es[hq * (b - 1) + 2 * x]], S["h_l%d" % b], T.dl[2 * b - 2 + x], T.hl[b - 1]) for x in range(2)])
+
     lists_in(1)
     g.wait_ge(S.v_lst, 1)
     fused(*[(cores[o[2 + i]], out_es[i * n_out // 2:(i + 1) * n_out // 2], S.l0, own_list(2 + i),
              T.off0[:, LC * i:LC * i + LC]) for i in range(2)])
     fused((cores[o[1]], out_es, S.ld, own_list(1), T.offd[:]))
+    lists_in(2)
     for b in range(3):
-        xc = 0 if carries_codes(0, b) else 1
         g.wait_ge(S["q_%d" % b], 1)
-        fused(*[(hs[side][xc], sides[side], S["h_%d" % b], codes(T["cb%d" % b], side), codes(T.hc, b)) for side in range(2)])
-        fused(*[(hs[side][1 - xc], sides[side], S["h_%d" % b], plane(T["pb%d" % b], side), plane(T.hp, b))
-                for side in range(2)])
-    g.wait_ge(S.q_d, 1)
-    fused((cores[o[1]], out_es, S.rd, codes(T.lc, 0), codes(T.lc, 2)))
-    fused((cores[o[1]], out_es, S.rd, plane(T.lp, 0), plane(T.lp, 2)))
+        for kind, ranks in CALLS[b]:
+            view, mine, theirs, sem = ((codes, "cb%d" % b, T.hc, "h_c%d" % b), (plane, "pb%d" % b, T.hp, "h_p%d" % b))[kind]
+            fused(*[(hs[WAY[b][i][kind][0]][WAY[b][i][kind][1]], sides[i] if len(ranks) > 1 else out_es + in_es, S[sem],
+                     view(T[mine], i), view(theirs, b)) for i in ranks])
+        if b == 2:
+            g.wait_ge(S.q_d, 1)
+            fused((cores[o[1]], out_es, S.rd, codes(T.cd, 1), codes(T.lc, 2)))
+            fused((cores[o[1]], out_es, S.rd, plane(T.pd, 1), plane(T.lp, 2)))
     g.wait_ge(S.sent, sent[0])
 
     v.wait_ge(S.d_rq, 16)
@@ -221,16 +232,14 @@ def rank_program(g, core, T, topo):
         v.wait_ge(sem, n)
         sc.wait_ge(sem, n)
 
-    def quantise(name, c, p, tile, a):
+    def quantise(name, c, p, tile, a, n=2 * W):
         v.wait_ge(S["v_g" + name], 2)
         v.wait_ge(S["s_g" + name], 2)
-        v.quantize_mx(T[c][:, 0:2 * W], T[p][:, 0:2 * W], T[tile][:, 4 * a:4 * a + 8 * W]).then_inc(S["q_" + name], 1)
+        v.quantize_mx(T[c][:, 0:n], T[p][:, 0:n], T[tile][:, 4 * a:4 * (a + n)]).then_inc(S["q_" + name], 1)
 
     both_wait(S.l0, n_out)
     gather("tb0", 0, 2 * W, T.off0[:], "0")
     quantise("0", "cb0", "pb0", "tb0", 0)
-    both_wait(S.v_lst, 1)
-    gather("tb2", 3 * W, 4 * W, own_list(0), "o")
     cast(1)
     both_wait(S.v_l1, 1)
     gather("tb1", 0, 2 * W, T.off1[:], "1")
@@ -241,16 +250,17 @@ def rank_program(g, core, T, topo):
     quantise("2", "cb2", "pb2", "tb2", 0)
     both_wait(S.ld, n_out)
     gather("tb2", 2 * W, 3 * W, T.offd[:], "d")
-    v.wait_ge(S.v_go, 2)
-    v.wait_ge(S.s_go, 2)
-    quantise("d", "lc", "lp", "tb2", 2 * W)
+    quantise("d", "cd", "pd", "tb2", W)
     v.wait_ge(S.d_qd, 16)
     v.quantize_mx(T.qc[:], T.qp[:], T.qt[:]).then_inc(S.q_q, 1)
+    both_wait(S.v_lst, 1)
+    gather("tb2", 3 * W, 4 * W, own_list(0), "o")
+    quantise("o", "lc", "lp", "tb2", 2 * W)
     v.wait_ge(S.d_od, 16)
     v.tensor_copy(T.offo[:], T.odi[:]).then_inc(S.v_od, 1)
 
     pe.wait_ge(S.q_q, 1)
-    steps = [(2, [("r0", 4 * n_out)]), (4, [("r1", 4 * n_out)]), (0, [("q_d", 1), ("rd", 2 * n_out)]), (6, [("r2", 4 * n_out)])]
+    steps = [(2, [("r0", 4 * n_out)]), (4, [("r1", 4 * n_out)]), (0, [("q_o", 1), ("rd", 2 * n_out)]), (6, [("r2", 4 * n_out)])]
     for j, (place, ready) in enumerate(steps):
         a = W * (place + 1)
         for s, cnt in ready:

import comms_topo
from concourse.bass import DstId, RemoteDMATransfer
from concourse.mybir import dt, ActivationFunctionType

N = 8
W = 64
LC = 4
COPY = ActivationFunctionType.Copy

SCRATCH = {
    "dl": ("dram", [4, 128, LC], "int32"),
    "hl": ("dram", [2, 128, LC], "int32"),
    "rqi": ("sbuf", [128, 32], "int32"),
    "lst": ("sbuf", [128, 32], "uint16"),
    "offi": ("sbuf", [128, 16], "int32"),
    "offd": ("sbuf", [128, LC], "uint16"),
    "off0": ("sbuf", [128, 8], "uint16"),
    "off1": ("sbuf", [128, 8], "uint16"),
    "off2": ("sbuf", [128, 8], "uint16"),
    "kyt": ("sbuf", [128, 2048], "bfloat16"),
    "kp0": ("sbuf", [128, 512], "bfloat16"),
    "kp1": ("sbuf", [128, 512], "bfloat16"),
    "kp2": ("sbuf", [128, 512], "bfloat16"),
    "kp3": ("sbuf", [128, 512], "bfloat16"),
    "tb0": ("sbuf", [128, 512], "bfloat16"),
    "tb1": ("sbuf", [128, 512], "bfloat16"),
    "tb2": ("sbuf", [128, 1024], "bfloat16"),
    "cd": ("sbuf", [128, 128], "float8_e4m3fn_x4"),
    "pd": ("sbuf", [128, 128], "uint8"),
    "cb0": ("sbuf", [128, 128], "float8_e4m3fn_x4"),
    "pb0": ("sbuf", [128, 128], "uint8"),
    "cb1": ("sbuf", [128, 128], "float8_e4m3fn_x4"),
    "pb1": ("sbuf", [128, 128], "uint8"),
    "cb2": ("sbuf", [128, 128], "float8_e4m3fn_x4"),
    "pb2": ("sbuf", [128, 128], "uint8"),
    "hc": ("sbuf", [128, 192], "float8_e4m3fn_x4"),
    "hp": ("sbuf", [128, 192], "uint8"),
    "qt": ("sbuf", [128, 1024], "bfloat16"),
    "qc": ("sbuf", [128, 256], "float8_e4m3fn_x4"),
    "qp": ("sbuf", [128, 256], "uint8"),
    "lc": ("sbuf", [128, 576], "float8_e4m3fn_x4"),
    "lp": ("sbuf", [128, 576], "uint8"),
    "ps": ("psum", [128, 4096], "float32"),
    "z0": ("sbuf", [128, 512], "float32"),
    "z1": ("sbuf", [128, 512], "float32"),
    "odi": ("sbuf", [128, 16], "int32"),
    "offo": ("sbuf", [128, 16], "uint16"),
    "y0": ("sbuf", [128, 256], "float32"),
    "y1": ("sbuf", [128, 256], "float32"),
}
SEMAPHORES = [
    "d_l1", "d_l2", "d_rq", "d_ky0", "d_ky1", "d_qd", "d_od", "d_y0", "d_y1",
    "v_lst", "v_l1", "v_l2", "v_od", "v_kp", "s_kp",
    "v_g0", "s_g0", "v_g1", "s_g1", "v_g2", "s_g2", "v_gd", "s_gd", "v_go", "s_go",
    "q_0", "q_1", "q_2", "q_d", "q_o", "q_q",
    "t0_0", "t0_1", "t0_2", "t0_3", "t1_0", "t1_1", "t1_2", "t1_3",
    "v_z", "s_z", "v_y0", "s_y0", "v_y1", "s_y1",
    "l0", "l1", "l2", "ld", "r0", "r1", "r2", "rd", "sent",
    "h_l1", "h_l2", "h_c0", "h_c1", "h_c2", "h_p0", "h_p1", "h_p2", "h_sent",
]


def order(core, T, topo):
    me = T.rank_of(core)
    cores = list(T.cores)
    same = [q for q in range(N) if q == me or topo.may_write(core, cores[q])]
    cross = [q for q in range(N) if q not in same]
    j = same.index(me)
    return [same[j ^ x] for x in range(4)] + [cross[j ^ x] for x in range(4)]


def helpers(core, T, topo):
    far = [list(T.cores)[q] for q in order(core, T, topo)[4:]]
    ok = [h for h in topo.cores_of(core) if h != core and all(topo.may_write(h, d) for d in far)]
    rest = [h for h in topo.cores_of(core) if h != core and h not in ok and topo.die(h) == topo.die(core)]
    return [[h for h in ok if topo.die(h) == topo.die(core)], [h for h in ok if topo.die(h) != topo.die(core)], rest]


def engine_sets(core, T, topo):
    out_es = topo.engines(core, list(T.cores)[order(core, T, topo)[1]])
    return out_es, [e for e in topo.engines(core, helpers(core, T, topo)[0][0]) if e not in out_es]


def bits(es):
    return sum(1 << e for e in es)


def transfer(topo, core, dst_core, es, sem, src, dst):
    rid, pid = topo.addr(dst_core, core)
    return RemoteDMATransfer(dst_ids=[DstId(rid=rid, pnc=pid)], dma_engine_mask=bits(es), remote_sem=sem, src=src, dst=dst)


def codes(buf, i):
    return buf[:, W * i:W * i + W].bitcast(dt.uint8)


def plane(buf, i):
    return buf[:, W * i:W * i + W]


WAY = ((((1, 0), (1, 1)), ((2, 0), (2, 0))),
       (((1, 0), (1, 1)), ((0, 0), (0, 1))),
       (((1, 0), (1, 1)), ((0, 0), (0, 1))))
CALLS = (((1, (0,)), (0, (0,)), (0, (1,)), (1, (1,))),
         ((0, (0, 1)), (1, (0, 1))),
         ((0, (0,)), (1, (0,)), (0, (1,)), (1, (1,))))


def helper_program(g, core, T, topo, owner, side, x):
    cores = list(T.cores)
    o = order(owner, T, topo)
    n_all = len(topo.engines(owner, core))
    sent = 0

    def send(place, dst, src, sem):
        d = cores[o[place]]
        rid, pid = topo.addr(d, core)
        g.remote_dma(dst, src, sem, T.sem.h_sent, pid, rid, topo.mask(core, d))
        return len(topo.engines(core, d))

    if side == 0:
        for b in (1, 2):
            i = 2 * b - 2 + x
            g.wait_ge(T.sem["h_l%d" % b], 1)
            sent += send(4 + i, T.offi[:, LC * i:LC * i + LC], T.hl[b - 1], T.sem["l%d" % b])
    for b in range(3):
        for kind, ranks in CALLS[b]:
            view, held, landing = ((codes, T.hc, T.lc), (plane, T.hp, T.lp))[kind]
            for i in ranks:
                if WAY[b][i][kind] == (side, x):
                    place = 2 + 2 * b + i
                    g.wait_ge(T.sem["h_%s%d" % ("cp"[kind], b)], n_all // len(ranks))
                    sent += send(place, view(landing, place + 1), view(held, b), T.sem["r%d" % b])
    g.wait_ge(T.sem.h_sent, sent)


def rank_program(g, core, T, topo):
    cores = list(T.cores)
    rank = T.rank_of(core)
    if rank is None:
        for owner in cores:
            if core in topo.cores_of(owner):
                hs = helpers(owner, T, topo)
                for side in range(3):
                    if core in hs[side]:
                        helper_program(g, core, T, topo, owner, side, hs[side].index(core))
        return

    o = order(core, T, topo)
    hs = helpers(core, T, topo)
    sides = engine_sets(core, T, topo)
    out_es, in_es = sides
    n_out, hq = len(out_es), len(in_es) // 2
    S = T.sem
    v, sc, pe, sy = g.vector, g.scalar, g.tensor, g.sync

    def park(queue, i):
        q = o[4 + i]
        queue.dma_start(T.dl[i], T.rq[:, LC * q:LC * q + LC]).then_inc(S["d_l%d" % (1 + i // 2)], 16)

    park(sy, 0)
    park(sc, 1)
    sy.dma_start(T.rqi[:], T.rq[:]).then_inc(S.d_rq, 16)
    sc.dma_start(T.kyt[:, 0:1024], T.ky[:, 0:1024]).then_inc(S.d_ky0, 16)
    sy.dma_start(T.kyt[:, 1024:2048], T.ky[:, 1024:2048]).then_inc(S.d_ky1, 16)
    park(sy, 2)
    park(sy, 3)
    sy.wait_ge(S.l0, n_out)
    sy.dma_start(T.qt[:], T.qd[:]).then_inc(S.d_qd, 16)
    sy.dma_start(T.odi[:], T.od[:]).then_inc(S.d_od, 16)

    sent = [0]

    def fused(*moves):
        g.remote_dma_fused([transfer(topo, core, *m) for m in moves], local_sem=S.sent)
        sent[0] += sum(len(m[1]) for m in moves)

    def own_list(place):
        return T.lst[:, LC * o[place]:LC * o[place] + LC]

    def lists_in(b):
        g.wait_ge(S["d_l%d" % b], 32)
        fused(*[(hs[0][x], [in_es[hq * (b - 1) + 2 * x]], S["h_l%d" % b], T.dl[2 * b - 2 + x], T.hl[b - 1]) for x in range(2)])

    lists_in(1)
    g.wait_ge(S.v_lst, 1)
    fused(*[(cores[o[2 + i]], out_es[i * n_out // 2:(i + 1) * n_out // 2], S.l0, own_list(2 + i),
             T.off0[:, LC * i:LC * i + LC]) for i in range(2)])
    fused((cores[o[1]], out_es, S.ld, own_list(1), T.offd[:]))
    lists_in(2)
    for b in range(3):
        g.wait_ge(S["q_%d" % b], 1)
        for kind, ranks in CALLS[b]:
            view, mine, theirs, sem = ((codes, "cb%d" % b, T.hc, "h_c%d" % b), (plane, "pb%d" % b, T.hp, "h_p%d" % b))[kind]
            fused(*[(hs[WAY[b][i][kind][0]][WAY[b][i][kind][1]], sides[i] if len(ranks) > 1 else out_es + in_es, S[sem],
                     view(T[mine], i), view(theirs, b)) for i in ranks])
        if b == 2:
            g.wait_ge(S.q_d, 1)
            fused((cores[o[1]], out_es, S.rd, codes(T.cd, 1), codes(T.lc, 2)))
            fused((cores[o[1]], out_es, S.rd, plane(T.pd, 1), plane(T.lp, 2)))
    g.wait_ge(S.sent, sent[0])

    v.wait_ge(S.d_rq, 16)
    v.tensor_copy(T.lst[:], T.rqi[:]).then_inc(S.v_lst, 1)

    for h in range(2):
        v.wait_ge(S["d_ky%d" % h], 16)
        for t in range(3):
            v.tensor_copy(T["kp%d" % t][:, 256 * h:256 * h + 256],
                          T.kyt[:, 1024 * h + t:1024 * h + 1024:4]).then_inc(S.v_kp, 1)
        sc.wait_ge(S["d_ky%d" % h], 16)
        sc.activation(T.kp3[:, 256 * h:256 * h + 256], T.kyt[:, 1024 * h + 3:1024 * h + 1024:4], COPY).then_inc(S.s_kp, 1)

    v.wait_ge(S.v_kp, 6)
    sc.wait_ge(S.v_kp, 6)
    sc.wait_ge(S.s_kp, 2)

    def gather(tile, a, b, offs, name, ts=range(4)):
        for t in ts:
            out = T[tile][:, 4 * a + t:4 * b:4]
            src = T["kp%d" % t][:, 0:512].indirect(offs)
            if t < 2:
                v.tensor_copy(out, src).then_inc(S["v_g" + name], 1)
            else:
                sc.activation(out, src, COPY).then_inc(S["s_g" + name], 1)

    def cast(b):
        v.wait_ge(S["l%d" % b], 2 * n_out)
        v.tensor_copy(T["off%d" % b][:], T.offi[:, 8 * b - 8:8 * b]).then_inc(S["v_l%d" % b], 1)

    def both_wait(sem, n):
        v.wait_ge(sem, n)
        sc.wait_ge(sem, n)

    def quantise(name, c, p, tile, a, n=2 * W):
        v.wait_ge(S["v_g" + name], 2)
        v.wait_ge(S["s_g" + name], 2)
        v.quantize_mx(T[c][:, 0:n], T[p][:, 0:n], T[tile][:, 4 * a:4 * (a + n)]).then_inc(S["q_" + name], 1)

    both_wait(S.l0, n_out)
    gather("tb0", 0, 2 * W, T.off0[:], "0")
    quantise("0", "cb0", "pb0", "tb0", 0)
    cast(1)
    both_wait(S.v_l1, 1)
    gather("tb1", 0, 2 * W, T.off1[:], "1")
    cast(2)
    quantise("1", "cb1", "pb1", "tb1", 0)
    both_wait(S.v_l2, 1)
    gather("tb2", 0, 2 * W, T.off2[:], "2")
    quantise("2", "cb2", "pb2", "tb2", 0)
    both_wait(S.ld, n_out)
    gather("tb2", 2 * W, 3 * W, T.offd[:], "d")
    quantise("d", "cd", "pd", "tb2", W)
    v.wait_ge(S.d_qd, 16)
    v.quantize_mx(T.qc[:], T.qp[:], T.qt[:]).then_inc(S.q_q, 1)
    both_wait(S.v_lst, 1)
    gather("tb2", 3 * W, 4 * W, own_list(0), "o")
    quantise("o", "lc", "lp", "tb2", 2 * W)
    v.wait_ge(S.d_od, 16)
    v.tensor_copy(T.offo[:], T.odi[:]).then_inc(S.v_od, 1)

    pe.wait_ge(S.q_q, 1)
    steps = [(2, [("r0", 4 * n_out)]), (4, [("r1", 4 * n_out)]), (0, [("q_o", 1), ("rd", 2 * n_out)]), (6, [("r2", 4 * n_out)])]
    for j, (place, ready) in enumerate(steps):
        a = W * (place + 1)
        for s, cnt in ready:
            pe.wait_ge(S[s], cnt)
        for t in range(2):
            bank = 512 * (4 * t + j)
            pe.matmul_mx(T.ps[:, bank:bank + 2 * W], T.qc[:, 128 * t:128 * t + 128], T.qp[:, 128 * t:128 * t + 128],
                         T.lc[:, a:a + 2 * W], T.lp[:, a:a + 2 * W], True, True).then_inc(S["t%d_%d" % (t, j)], 1)
        v.wait_ge(S["t0_%d" % j], 1)
        sc.wait_ge(S["t1_%d" % j], 1)
        for i in range(2):
            q = o[place + i]
            v.tensor_copy(T.z0[:, W * q:W * q + W], T.ps[:, 512 * j + W * i:512 * j + W * i + W]).then_inc(S.v_z, 1)
            sc.activation(T.z1[:, W * q:W * q + W], T.ps[:, 512 * (4 + j) + W * i:512 * (4 + j) + W * i + W],
                          COPY).then_inc(S.s_z, 1)

    both_wait(S.v_od, 1)
    for t, zs in enumerate((S.v_z, S.s_z)):
        z, y = T["z%d" % t], T["y%d" % t]
        both_wait(zs, N)
        v.tensor_copy(y[:, 0:128], z[:, 0:512].indirect(T.offo[:, 0:8])).then_inc(S["v_y%d" % t], 1)
        sc.activation(y[:, 128:256], z[:, 0:512].indirect(T.offo[:, 8:16]), COPY).then_inc(S["s_y%d" % t], 1)
    for t, queue in enumerate((sy, sc)):
        queue.wait_ge(S["v_y%d" % t], 1)
        queue.wait_ge(S["s_y%d" % t], 1)
        queue.dma_start(T.y[:, 256 * t:256 * t + 256], T["y%d" % t][:]).then_inc(S["d_y%d" % t], 16)
        queue.wait_ge(S["d_y%d" % t], 16)
